import numpy as np
import ml_dtypes


def mxq(x, axis, fmt="e4m3"):
    dtype, down = {"e4m3": (ml_dtypes.float8_e4m3fn, 7), "e5m2": (ml_dtypes.float8_e5m2, 14)}[fmt]
    v = np.moveaxis(np.asarray(x, np.float32).astype(ml_dtypes.bfloat16).astype(np.float64), axis, -1)
    blocks = v.reshape(v.shape[:-1] + (-1, 32))
    amax = np.abs(blocks).max(-1, keepdims=True)
    byte = np.maximum(np.where(amax > 0, np.frexp(amax)[1] - 1 + 127, 0) - down, 1)
    scale = np.exp2(byte - 127.0)
    codes = (blocks / scale).astype(np.float32).astype(dtype).astype(np.float64)
    return np.moveaxis((codes * scale).reshape(v.shape), -1, axis)


WIDE = False


def mx_kscale(k):
    if not WIDE:
        return np.ones(k)
    levels = np.array([10, -10, 5, -5, 0])
    if k % 512:
        return np.exp2(np.random.permutation(np.resize(levels, k // 32))).repeat(32)
    a = np.empty((k // 512, 16))
    for p in range(k // 512):
        a[p, :8] = np.random.permutation(np.resize(levels, 8))
        for g in range(8):
            far = levels[np.abs(levels - a[p, g]) >= 10]
            a[p, g + 8] = far[np.random.randint(len(far))]
    return np.exp2(a.ravel()).repeat(32)


def f64(x):
    return np.asarray(x).astype(np.float64)


def striped(idx):
    return np.tile(idx.reshape(-1, 16).T, (8, 1)).astype(np.uint16)


def unstriped(offs):
    return offs[:16].T.reshape(-1).astype(np.int64)


def pack_weight(w):
    k, n = w.shape
    w = f64(np.asarray(w, np.float32).astype(ml_dtypes.bfloat16)).reshape(k // 32, 32, n)
    amax = np.abs(w).max(1)
    byte = np.clip(np.where(amax > 0, np.frexp(amax)[1] - 1 + 127 - 7, 1), 1, 254)
    scaled = (w * np.exp2(127.0 - byte)[:, None, :]).reshape(k, n).astype(np.float32)
    words = np.ascontiguousarray(scaled.reshape(k // 512, 128, 4, n).transpose(0, 1, 3, 2)).astype(ml_dtypes.float8_e4m3fn).view(np.uint8)
    return words, np.ascontiguousarray(byte.astype(np.uint8).reshape(k // 512, 16, n))


def unpack_weight(words, scales):
    g, p, n, _ = words.shape
    vals = np.ascontiguousarray(words).view(ml_dtypes.float8_e4m3fn).astype(np.float64) * np.repeat(np.exp2(scales.astype(np.float64) - 127.0), 8, axis=1)[..., None]
    return vals.transpose(0, 1, 3, 2).reshape(g * 512, n)


def relu2(v):
    return np.maximum(v, 0.0) ** 2


K, T, S, V = 1024, 1024, 512, 512


def setup_inputs():
    n = np.random.standard_normal
    s = mx_kscale(K)[:, None]
    packed_xT = pack_weight(n((K, T)) * s)
    return {
        "x_words": packed_xT[0],
        "x_scales": packed_xT[1],
        "hT": (n((K, V)) / np.sqrt(K) / s).astype(np.float32),
        "offs": striped(np.random.permutation(T)[:S]),
    }


def reference(x_words, x_scales, hT, offs):
    hTq = mxq(f64(hT), 0, "e4m3")
    xq = unpack_weight(x_words, x_scales)[:, unstriped(offs)]
    y = hTq.T @ xq
    ex = np.exp(y - y.max(axis=1, keepdims=True))
    p = ex / ex.sum(axis=1, keepdims=True)
    top = p.max(axis=1, keepdims=True)
    rr = relu2(p - (0.01 * top))
    total = rr.sum(axis=1, keepdims=True)
    return rr / total

@@ -1,0 +1,126 @@
+from contextlib import ExitStack
+
+import concourse.mybir as mybir
+
+K, T, S, V = 1024, 1024, 512, 512
+FLOPS = 2 * K * S * V
+
+F32 = mybir.dt.float32
+BF16 = mybir.dt.bfloat16
+I32 = mybir.dt.int32
+U32 = mybir.dt.uint32
+U16 = mybir.dt.uint16
+U8 = mybir.dt.uint8
+FP8X4 = mybir.dt.float8_e4m3fn_x4
+ALU = mybir.AluOpType
+ACT = mybir.ActivationFunctionType
+AXIS = mybir.AxisListType
+
+P = 128
+PACK = 4
+K_PASS = P * PACK
+PASSES = K // K_PASS
+TILES = V // P
+SHARE = 0.01
+VECTOR_COPIES = [(3, 1), (2, 1)]
+
+
+def tile_picked_yminp_sq_p_kernel(tc, x_words, x_scales, hT, offs, out):
+    nc = tc.nc
+    with ExitStack() as ctx:
+        keep = ctx.enter_context(tc.tile_pool(name="keep", bufs=1))
+        psum = ctx.enter_context(tc.psum_pool(name="psum", bufs=1))
+
+        offsets = keep.tile([P, S // 16], U16, name="offsets")
+        nc.sync.dma_start(offsets[:], offs)
+
+        table_scales = keep.tile([P, T], U8, name="table_scales", align_bytes=64)
+        nc.gpsimd.memset(table_scales[:].bitcast(I32), 0)
+        for q in range(4):
+            nc.gpsimd.dma_start(
+                out=table_scales[32 * q : 32 * q + 4 * PASSES, :].bitcast(I32),
+                in_=x_scales[:, 4 * q : 4 * q + 4, :].bitcast(I32),
+            )
+
+        table_words = [keep.tile([P, T], I32, name=f"table_words{g}", align_bytes=64) for g in range(PASSES)]
+        raw = [[keep.tile([P, PACK, P], F32, name=f"raw{i}_{g}", align_bytes=64) for g in range(PASSES)] for i in range(TILES)]
+
+        def load_words(g):
+            nc.sync.dma_start(out=table_words[g][:], in_=x_words[g].rearrange("p n t -> p (n t)").bitcast(I32))
+
+        def load_hidden(i):
+            for g in range(PASSES):
+                rows = hT[g * K_PASS : (g + 1) * K_PASS, i * P : (i + 1) * P]
+                nc.sync.dma_start(out=raw[i][g][:], in_=rows.rearrange("(p j) w -> p j w", j=PACK))
+
+        load_hidden(0)
+        load_words(0)
+        load_words(1)
+        load_hidden(1)
+        load_hidden(2)
+        load_hidden(3)
+
+        picked_scales = keep.tile([P, S], U8, name="picked_scales", align_bytes=64)
+        picked_words = [keep.tile([P, S], U32, name=f"picked_words{g}", align_bytes=64) for g in range(PASSES)]
+        grouped = [[keep.tile([P, P, PACK], BF16, name=f"grouped{i}_{g}", align_bytes=64) for g in range(PASSES)] for i in range(TILES)]
+        h_codes = [[keep.tile([P, P], U32, name=f"h_codes{i}_{g}", align_bytes=64) for g in range(PASSES)] for i in range(TILES)]
+        h_scales = [[keep.tile([P, P], U8, name=f"h_scales{i}_{g}", align_bytes=64) for g in range(PASSES)] for i in range(TILES)]
+        logits = [psum.tile([P, S], F32, name=f"logits{i}") for i in range(TILES)]
+
+        def interleave(i):
+            for g in range(PASSES):
+                dst = grouped[i][g][:].rearrange("p (c u) j -> p c j u", u=4)
+                src = raw[i][g][:].rearrange("p j (c u) -> p c j u", u=4)
+                if (i, g) in VECTOR_COPIES:
+                    nc.vector.tensor_copy(out=dst, in_=src)
+                else:
+                    nc.scalar.activation(out=dst, in_=src, func=ACT.Copy)
+
+        def quantize(i):
+            for g in range(PASSES):
+                nc.vector.quantize_mx(
+                    out=h_codes[i][g][:].bitcast(FP8X4),
+                    scales=h_scales[i][g][:],
+                    in_=grouped[i][g][:].rearrange("p c j -> p (c j)"),
+                )
+
+        def multiply(i):
+            for g in range(PASSES):
+                nc.tensor.matmul_mx(
+                    out=logits[i][:],
+                    lhsT=h_codes[i][g][:].bitcast(FP8X4),
+                    lhsT_scale=h_scales[i][g][:],
+                    rhs=picked_words[g][:].bitcast(FP8X4),
+                    rhs_scale=picked_scales[4 * g : P, :],
+                    start=(g == 0),
+                    stop=(g == PASSES - 1),
+                )
+
+        def finish(i):
+            neg_max = keep.tile([P, 1], F32, name=f"neg_max{i}")
+            nc.vector.tensor_reduce(out=neg_max[:], in_=logits[i][:], axis=AXIS.X, op=ALU.max, negate=True)
+            expd = keep.tile([P, S], F32, name=f"expd{i}")
+            nc.scalar.activation(out=expd[:], in_=logits[i][:], func=ACT.Exp, bias=neg_max[:], scale=1.0)
+            kept = keep.tile([P, S], F32, name=f"kept{i}")
+            nc.vector.tensor_scalar(out=kept[:], in0=expd[:], scalar1=-SHARE, scalar2=0.0, op0=ALU.add, op1=ALU.max)
+            squares = keep.tile([P, S], F32, name=f"squares{i}")
+            total = keep.tile([P, 1], F32, name=f"total{i}")
+            nc.scalar.activation(out=squares[:], in_=kept[:], func=ACT.Square, accum_out=total[:])
+            inverse = keep.tile([P, 1], F32, name=f"inverse{i}")
+            nc.vector.reciprocal(out=inverse[:], in_=total[:])
+            result = keep.tile([P, S], F32, name=f"result{i}")
+            nc.vector.tensor_scalar(out=result[:], in0=squares[:], scalar1=inverse[:], scalar2=None, op0=ALU.mult)
+            nc.sync.dma_start(out=out[i * P : (i + 1) * P, :], in_=result[:])
+
+        nc.vector.tensor_copy(out=picked_scales[:], in_=table_scales[:].indirect(offsets[:]))
+        interleave(0)
+        nc.vector.tensor_copy(out=picked_words[0][:], in_=table_words[0][:].bitcast(U32).indirect(offsets[:]))
+        quantize(0)
+        nc.vector.tensor_copy(out=picked_words[1][:], in_=table_words[1][:].bitcast(U32).indirect(offsets[:]))
+        multiply(0)
+        for i in range(1, TILES):
+            interleave(i)
+            quantize(i)
+            multiply(i)
+            finish(i - 1)
+        finish(TILES - 1)

@@ -21,106 +21,143 @@ PACK = 4
 K_PASS = P * PACK
 PASSES = K // K_PASS
 TILES = V // P
+QUADRANTS, QUADRANT = 4, 32
+SCALE_ROWS = 4
+RUN = 4
 SHARE = 0.01
-VECTOR_COPIES = [(3, 1), (2, 1)]
+ALIGN = 64
+
+LAG_EXP, LAG_THRESHOLD, LAG_SQUARE, LAG_STORE = 1, 2, 3, 4
 
 
 def tile_picked_yminp_sq_p_kernel(tc, x_words, x_scales, hT, offs, out):
     nc = tc.nc
     with ExitStack() as ctx:
-        keep = ctx.enter_context(tc.tile_pool(name="keep", bufs=1))
+        sbuf = ctx.enter_context(tc.tile_pool(name="sbuf", bufs=1))
         psum = ctx.enter_context(tc.psum_pool(name="psum", bufs=1))
+        made = {}
 
-        offsets = keep.tile([P, S // 16], U16, name="offsets")
+        def new(kind, key, shape, dtype, tag=None):
+            name = f"{kind}_{key}"
+            made[kind, key] = sbuf.tile(shape, dtype, name=name, tag=tag or name, align_bytes=ALIGN)
+            return made[kind, key]
+
+        offsets = sbuf.tile([P, S // 16], U16, name="offsets")
         nc.sync.dma_start(offsets[:], offs)
 
-        table_scales = keep.tile([P, T], U8, name="table_scales", align_bytes=64)
+        table_scales = sbuf.tile([P, T], U8, name="table_scales", align_bytes=ALIGN)
         nc.gpsimd.memset(table_scales[:].bitcast(I32), 0)
-        for q in range(4):
-            nc.gpsimd.dma_start(
-                out=table_scales[32 * q : 32 * q + 4 * PASSES, :].bitcast(I32),
-                in_=x_scales[:, 4 * q : 4 * q + 4, :].bitcast(I32),
-            )
+        picked_scales = sbuf.tile([P, S], U8, name="picked_scales", align_bytes=ALIGN)
+        logits = [psum.tile([P, S], F32, name=f"logits_{i}") for i in range(TILES)]
 
-        table_words = [keep.tile([P, T], I32, name=f"table_words{g}", align_bytes=64) for g in range(PASSES)]
-        raw = [[keep.tile([P, PACK, P], F32, name=f"raw{i}_{g}", align_bytes=64) for g in range(PASSES)] for i in range(TILES)]
+        def load_scales():
+            for q in range(QUADRANTS):
+                nc.sync.dma_start(
+                    out=table_scales[QUADRANT * q : QUADRANT * q + SCALE_ROWS * PASSES, :].bitcast(I32),
+                    in_=x_scales[:, SCALE_ROWS * q : SCALE_ROWS * (q + 1), :].bitcast(I32),
+                )
 
         def load_words(g):
-            nc.sync.dma_start(out=table_words[g][:], in_=x_words[g].rearrange("p n t -> p (n t)").bitcast(I32))
+            words = new("table_words", g, [P, T], I32)
+            nc.sync.dma_start(out=words[:], in_=x_words[g].rearrange("p n j -> p (n j)").bitcast(I32))
 
-        def load_hidden(i):
-            for g in range(PASSES):
-                rows = hT[g * K_PASS : (g + 1) * K_PASS, i * P : (i + 1) * P]
-                nc.sync.dma_start(out=raw[i][g][:], in_=rows.rearrange("(p j) w -> p j w", j=PACK))
+        def load_hidden(i, g):
+            raw = new("raw", PASSES * i + g, [P, PACK, P], F32)
+            rows = hT[g * K_PASS : (g + 1) * K_PASS, i * P : (i + 1) * P]
+            nc.sync.dma_start(out=raw[:], in_=rows.rearrange("(p j) c -> p j c", j=PACK))
 
-        load_hidden(0)
-        load_words(0)
-        load_words(1)
-        load_hidden(1)
-        load_hidden(2)
-        load_hidden(3)
+        def gather_words(g):
+            picked = new("picked_words", g, [P, S], U32)
+            nc.vector.tensor_copy(out=picked[:], in_=made["table_words", g][:].bitcast(U32).indirect(offsets[:]))
 
-        picked_scales = keep.tile([P, S], U8, name="picked_scales", align_bytes=64)
-        picked_words = [keep.tile([P, S], U32, name=f"picked_words{g}", align_bytes=64) for g in range(PASSES)]
-        grouped = [[keep.tile([P, P, PACK], BF16, name=f"grouped{i}_{g}", align_bytes=64) for g in range(PASSES)] for i in range(TILES)]
-        h_codes = [[keep.tile([P, P], U32, name=f"h_codes{i}_{g}", align_bytes=64) for g in range(PASSES)] for i in range(TILES)]
-        h_scales = [[keep.tile([P, P], U8, name=f"h_scales{i}_{g}", align_bytes=64) for g in range(PASSES)] for i in range(TILES)]
-        logits = [psum.tile([P, S], F32, name=f"logits{i}") for i in range(TILES)]
+        def interleave(i, g):
+            grouped = new("grouped", PASSES * i + g, [P, P, PACK], BF16)
+            dst = grouped[:].rearrange("p (c u) j -> p c j u", u=RUN)
+            src = made["raw", PASSES * i + g][:].rearrange("p j (c u) -> p c j u", u=RUN)
+            if (i, g) == (TILES - 1, PASSES - 1):
+                nc.vector.tensor_copy(out=dst, in_=src)
+            else:
+                nc.scalar.activation(out=dst, in_=src, func=ACT.Copy)
 
-        def interleave(i):
-            for g in range(PASSES):
-                dst = grouped[i][g][:].rearrange("p (c u) j -> p c j u", u=4)
-                src = raw[i][g][:].rearrange("p j (c u) -> p c j u", u=4)
-                if (i, g) in VECTOR_COPIES:
-                    nc.vector.tensor_copy(out=dst, in_=src)
-                else:
-                    nc.scalar.activation(out=dst, in_=src, func=ACT.Copy)
-
-        def quantize(i):
-            for g in range(PASSES):
-                nc.vector.quantize_mx(
-                    out=h_codes[i][g][:].bitcast(FP8X4),
-                    scales=h_scales[i][g][:],
-                    in_=grouped[i][g][:].rearrange("p c j -> p (c j)"),
-                )
+        def quantize(i, g):
+            codes = new("codes", PASSES * i + g, [P, P], U32)
+            scales = new("scales", PASSES * i + g, [P, P], U8)
+            nc.vector.quantize_mx(
+                out=codes[:].bitcast(FP8X4),
+                scales=scales[:],
+                in_=made["grouped", PASSES * i + g][:].rearrange("p c j -> p (c j)"),
+            )
 
         def multiply(i):
             for g in range(PASSES):
                 nc.tensor.matmul_mx(
                     out=logits[i][:],
-                    lhsT=h_codes[i][g][:].bitcast(FP8X4),
-                    lhsT_scale=h_scales[i][g][:],
-                    rhs=picked_words[g][:].bitcast(FP8X4),
-                    rhs_scale=picked_scales[4 * g : P, :],
+                    lhsT=made["codes", PASSES * i + g][:].bitcast(FP8X4),
+                    lhsT_scale=made["scales", PASSES * i + g][:],
+                    rhs=made["picked_words", g][:].bitcast(FP8X4),
+                    rhs_scale=picked_scales[SCALE_ROWS * g : P, :],
                     start=(g == 0),
                     stop=(g == PASSES - 1),
                 )
 
-        def finish(i):
-            neg_max = keep.tile([P, 1], F32, name=f"neg_max{i}")
+        def row_max(i):
+            reuse = f"raw_{PASSES * (i + 2) - 1}" if i + 1 < TILES else None
+            neg_max = new("neg_max", i, [P, 1], F32, tag=reuse)
             nc.vector.tensor_reduce(out=neg_max[:], in_=logits[i][:], axis=AXIS.X, op=ALU.max, negate=True)
-            expd = keep.tile([P, S], F32, name=f"expd{i}")
-            nc.scalar.activation(out=expd[:], in_=logits[i][:], func=ACT.Exp, bias=neg_max[:], scale=1.0)
-            kept = keep.tile([P, S], F32, name=f"kept{i}")
-            nc.vector.tensor_scalar(out=kept[:], in0=expd[:], scalar1=-SHARE, scalar2=0.0, op0=ALU.add, op1=ALU.max)
-            squares = keep.tile([P, S], F32, name=f"squares{i}")
-            total = keep.tile([P, 1], F32, name=f"total{i}")
-            nc.scalar.activation(out=squares[:], in_=kept[:], func=ACT.Square, accum_out=total[:])
-            inverse = keep.tile([P, 1], F32, name=f"inverse{i}")
-            nc.vector.reciprocal(out=inverse[:], in_=total[:])
-            result = keep.tile([P, S], F32, name=f"result{i}")
-            nc.vector.tensor_scalar(out=result[:], in0=squares[:], scalar1=inverse[:], scalar2=None, op0=ALU.mult)
+
+        def exponential(i):
+            exps = new("exps", i, [P, S], F32)
+            nc.scalar.activation(out=exps[:], in_=logits[i][:], func=ACT.Exp, bias=made["neg_max", i][:], scale=1.0)
+
+        def threshold(i):
+            kept = new("kept", i, [P, S], F32)
+            nc.vector.tensor_scalar(
+                out=kept[:], in0=made["exps", i][:], scalar1=-SHARE, scalar2=0.0, op0=ALU.add, op1=ALU.max
+            )
+
+        def square(i):
+            squares = new("squares", i, [P, S], F32)
+            total = new("total", i, [P, 1], F32)
+            nc.scalar.activation(out=squares[:], in_=made["kept", i][:], func=ACT.Square, accum_out=total[:])
+
+        def invert_total(i):
+            inverse = new("inverse", i, [P, 1], F32)
+            nc.vector.reciprocal(out=inverse[:], in_=made["total", i][:])
+
+        def normalise_and_store(i):
+            result = new("result", i, [P, S], F32)
+            nc.vector.tensor_scalar(
+                out=result[:], in0=made["squares", i][:], scalar1=made["inverse", i][:], scalar2=None, op0=ALU.mult
+            )
             nc.sync.dma_start(out=out[i * P : (i + 1) * P, :], in_=result[:])
 
+        load_hidden(0, 0)
+        load_scales()
+        for g in range(PASSES):
+            load_words(g)
+        for block in range(1, TILES * PASSES):
+            load_hidden(block // PASSES, block % PASSES)
+
         nc.vector.tensor_copy(out=picked_scales[:], in_=table_scales[:].indirect(offsets[:]))
-        interleave(0)
-        nc.vector.tensor_copy(out=picked_words[0][:], in_=table_words[0][:].bitcast(U32).indirect(offsets[:]))
-        quantize(0)
-        nc.vector.tensor_copy(out=picked_words[1][:], in_=table_words[1][:].bitcast(U32).indirect(offsets[:]))
+        for g in range(PASSES):
+            interleave(0, g)
+            gather_words(g)
+            quantize(0, g)
         multiply(0)
-        for i in range(1, TILES):
-            interleave(i)
-            quantize(i)
-            multiply(i)
-            finish(i - 1)
-        finish(TILES - 1)
+
+        def run(stage, i, *rest):
+            if 0 <= i < TILES:
+                stage(i, *rest)
+
+        for n in range(1, TILES + LAG_STORE):
+            run(invert_total, n - LAG_STORE)
+            run(interleave, n, 0)
+            run(interleave, n, 1)
+            run(quantize, n, 0)
+            run(threshold, n - LAG_THRESHOLD)
+            run(quantize, n, 1)
+            run(multiply, n)
+            run(row_max, n - LAG_EXP)
+            run(normalise_and_store, n - LAG_STORE)
+            run(exponential, n - LAG_EXP)
+            run(square, n - LAG_SQUARE)

@@ -48,7 +48,11 @@ def tile_picked_yminp_sq_p_kernel(tc, x_words, x_scales, hT, offs, out):
         table_scales = sbuf.tile([P, T], U8, name="table_scales", align_bytes=ALIGN)
         nc.gpsimd.memset(table_scales[:].bitcast(I32), 0)
         picked_scales = sbuf.tile([P, S], U8, name="picked_scales", align_bytes=ALIGN)
-        logits = [psum.tile([P, S], F32, name=f"logits_{i}") for i in range(TILES)]
+        spans = [[slice(h * S // 2, (h + 1) * S // 2) for h in range(2)]] + [[slice(0, S)]] * (TILES - 1)
+        logits = [
+            [psum.tile([P, cols.stop - cols.start], F32, name=f"logits_{i}_{cols.start}") for cols in spans[i]]
+            for i in range(TILES)
+        ]
 
         def load_scales():
             for q in range(QUADRANTS):
@@ -68,7 +72,9 @@ def tile_picked_yminp_sq_p_kernel(tc, x_words, x_scales, hT, offs, out):
 
         def gather_words(g):
             picked = new("picked_words", g, [P, S], U32)
-            nc.vector.tensor_copy(out=picked[:], in_=made["table_words", g][:].bitcast(U32).indirect(offsets[:]))
+            for cols in spans[0] if g == PASSES - 1 else spans[1]:
+                entries = offsets[:, cols.start // 16 : cols.stop // 16]
+                nc.vector.tensor_copy(out=picked[:, cols], in_=made["table_words", g][:].bitcast(U32).indirect(entries))
 
         def interleave(i, g):
             grouped = new("grouped", PASSES * i + g, [P, P, PACK], BF16)
@@ -90,24 +96,34 @@ def tile_picked_yminp_sq_p_kernel(tc, x_words, x_scales, hT, offs, out):
 
         def multiply(i):
             for g in range(PASSES):
-                nc.tensor.matmul_mx(
-                    out=logits[i][:],
-                    lhsT=made["codes", PASSES * i + g][:].bitcast(FP8X4),
-                    lhsT_scale=made["scales", PASSES * i + g][:],
-                    rhs=made["picked_words", g][:].bitcast(FP8X4),
-                    rhs_scale=picked_scales[SCALE_ROWS * g : P, :],
-                    start=(g == 0),
-                    stop=(g == PASSES - 1),
-                )
+                for bank, cols in zip(logits[i], spans[i]):
+                    nc.tensor.matmul_mx(
+                        out=bank[:],
+                        lhsT=made["codes", PASSES * i + g][:].bitcast(FP8X4),
+                        lhsT_scale=made["scales", PASSES * i + g][:],
+                        rhs=made["picked_words", g][:, cols].bitcast(FP8X4),
+                        rhs_scale=picked_scales[SCALE_ROWS * g : P, cols],
+                        start=(g == 0),
+                        stop=(g == PASSES - 1),
+                    )
 
         def row_max(i):
             reuse = f"raw_{PASSES * (i + 2) - 1}" if i + 1 < TILES else None
-            neg_max = new("neg_max", i, [P, 1], F32, tag=reuse)
-            nc.vector.tensor_reduce(out=neg_max[:], in_=logits[i][:], axis=AXIS.X, op=ALU.max, negate=True)
+            neg_max = new("neg_max", i, [P, 1], F32, tag=reuse if len(logits[i]) == 1 else None)
+            if len(logits[i]) == 1:
+                nc.vector.tensor_reduce(out=neg_max[:], in_=logits[i][0][:], axis=AXIS.X, op=ALU.max, negate=True)
+                return
+            partial = new("partial_max", i, [P, len(logits[i])], F32, tag=reuse)
+            for h, bank in enumerate(logits[i]):
+                nc.vector.tensor_reduce(out=partial[:, h : h + 1], in_=bank[:], axis=AXIS.X, op=ALU.max)
+            nc.vector.tensor_reduce(out=neg_max[:], in_=partial[:], axis=AXIS.X, op=ALU.max, negate=True)
 
         def exponential(i):
             exps = new("exps", i, [P, S], F32)
-            nc.scalar.activation(out=exps[:], in_=logits[i][:], func=ACT.Exp, bias=made["neg_max", i][:], scale=1.0)
+            for bank, cols in zip(logits[i], spans[i]):
+                nc.scalar.activation(
+                    out=exps[:, cols], in_=bank[:], func=ACT.Exp, bias=made["neg_max", i][:], scale=1.0
+                )
 
         def threshold(i):
             kept = new("kept", i, [P, S], F32)
@@ -125,24 +141,34 @@ def tile_picked_yminp_sq_p_kernel(tc, x_words, x_scales, hT, offs, out):
             nc.vector.reciprocal(out=inverse[:], in_=made["total", i][:])
 
         def normalise_and_store(i):
-            result = new("result", i, [P, S], F32)
-            nc.vector.tensor_scalar(
-                out=result[:], in0=made["squares", i][:], scalar1=made["inverse", i][:], scalar2=None, op0=ALU.mult
-            )
-            nc.sync.dma_start(out=out[i * P : (i + 1) * P, :], in_=result[:])
+            parts = 2 if i == TILES - 1 else 1
+            for part in range(parts):
+                cols = slice(part * S // parts, (part + 1) * S // parts)
+                result = new("result", f"{i}_{part}", [P, S // parts], F32)
+                nc.vector.tensor_scalar(
+                    out=result[:],
+                    in0=made["squares", i][:, cols],
+                    scalar1=made["inverse", i][:],
+                    scalar2=None,
+                    op0=ALU.mult,
+                )
+                nc.sync.dma_start(out=out[i * P : (i + 1) * P, cols], in_=result[:])
 
         load_hidden(0, 0)
         load_scales()
-        for g in range(PASSES):
-            load_words(g)
-        for block in range(1, TILES * PASSES):
+        load_words(0)
+        load_hidden(0, 1)
+        load_words(1)
+        for block in range(PASSES, TILES * PASSES):
             load_hidden(block // PASSES, block % PASSES)
 
         nc.vector.tensor_copy(out=picked_scales[:], in_=table_scales[:].indirect(offsets[:]))
-        for g in range(PASSES):
-            interleave(0, g)
-            gather_words(g)
-            quantize(0, g)
+        interleave(0, 0)
+        gather_words(0)
+        quantize(0, 0)
+        interleave(0, 1)
+        quantize(0, 1)
+        gather_words(1)
         multiply(0)
 
         def run(stage, i, *rest):

@@ -25,6 +25,7 @@ QUADRANTS, QUADRANT = 4, 32
 SCALE_ROWS = 4
 RUN = 4
 SHARE = 0.01
+LAST_ON_VECTOR = 88
 ALIGN = 64
 
 LAG_EXP, LAG_THRESHOLD, LAG_SQUARE, LAG_STORE = 1, 2, 3, 4
@@ -80,10 +81,10 @@ def tile_picked_yminp_sq_p_kernel(tc, x_words, x_scales, hT, offs, out):
             grouped = new("grouped", PASSES * i + g, [P, P, PACK], BF16)
             dst = grouped[:].rearrange("p (c u) j -> p c j u", u=RUN)
             src = made["raw", PASSES * i + g][:].rearrange("p j (c u) -> p c j u", u=RUN)
-            if (i, g) == (TILES - 1, PASSES - 1):
-                nc.vector.tensor_copy(out=dst, in_=src)
-            else:
-                nc.scalar.activation(out=dst, in_=src, func=ACT.Copy)
+            split = LAST_ON_VECTOR // RUN if (i, g) == (TILES - 1, PASSES - 1) else 0
+            if split:
+                nc.vector.tensor_copy(out=dst[:, :split], in_=src[:, :split])
+            nc.scalar.activation(out=dst[:, split:], in_=src[:, split:], func=ACT.Copy)
 
         def quantize(i, g):
             codes = new("codes", PASSES * i + g, [P, P], U32)

@@ -81,7 +81,7 @@ def tile_picked_yminp_sq_p_kernel(tc, x_words, x_scales, hT, offs, out):
             grouped = new("grouped", PASSES * i + g, [P, P, PACK], BF16)
             dst = grouped[:].rearrange("p (c u) j -> p c j u", u=RUN)
             src = made["raw", PASSES * i + g][:].rearrange("p j (c u) -> p c j u", u=RUN)
-            split = LAST_ON_VECTOR // RUN if (i, g) == (TILES - 1, PASSES - 1) else 0
+            split = LAST_ON_VECTOR // RUN if i == TILES - 1 else 0
             if split:
                 nc.vector.tensor_copy(out=dst[:, :split], in_=src[:, :split])
             nc.scalar.activation(out=dst[:, split:], in_=src[:, split:], func=ACT.Copy)

@@ -81,7 +81,7 @@ def tile_picked_yminp_sq_p_kernel(tc, x_words, x_scales, hT, offs, out):
             grouped = new("grouped", PASSES * i + g, [P, P, PACK], BF16)
             dst = grouped[:].rearrange("p (c u) j -> p c j u", u=RUN)
             src = made["raw", PASSES * i + g][:].rearrange("p j (c u) -> p c j u", u=RUN)
-            split = LAST_ON_VECTOR // RUN if i == TILES - 1 else 0
+            split = LAST_ON_VECTOR // RUN if i == TILES - 1 or (i, g) == (1, PASSES - 1) else 0
             if split:
                 nc.vector.tensor_copy(out=dst[:, :split], in_=src[:, :split])
             nc.scalar.activation(out=dst[:, split:], in_=src[:, split:], func=ACT.Copy)
@@ -176,14 +176,15 @@ def tile_picked_yminp_sq_p_kernel(tc, x_words, x_scales, hT, offs, out):
             if 0 <= i < TILES:
                 stage(i, *rest)
 
+        for n in range(1, TILES):
+            for g in range(PASSES):
+                interleave(n, g)
+            for g in range(PASSES):
+                quantize(n, g)
+            multiply(n)
         for n in range(1, TILES + LAG_STORE):
             run(invert_total, n - LAG_STORE)
-            run(interleave, n, 0)
-            run(interleave, n, 1)
-            run(quantize, n, 0)
             run(threshold, n - LAG_THRESHOLD)
-            run(quantize, n, 1)
-            run(multiply, n)
             run(row_max, n - LAG_EXP)
             run(normalise_and_store, n - LAG_STORE)
             run(exponential, n - LAG_EXP)

@@ -81,7 +81,10 @@ def tile_picked_yminp_sq_p_kernel(tc, x_words, x_scales, hT, offs, out):
             grouped = new("grouped", PASSES * i + g, [P, P, PACK], BF16)
             dst = grouped[:].rearrange("p (c u) j -> p c j u", u=RUN)
             src = made["raw", PASSES * i + g][:].rearrange("p j (c u) -> p c j u", u=RUN)
-            split = LAST_ON_VECTOR // RUN if i == TILES - 1 or (i, g) == (1, PASSES - 1) else 0
+            if (i, g) == (1, PASSES - 1):
+                nc.vector.tensor_copy(out=dst, in_=src)
+                return
+            split = LAST_ON_VECTOR // RUN if i == TILES - 1 else 0
             if split:
                 nc.vector.tensor_copy(out=dst[:, :split], in_=src[:, :split])
             nc.scalar.activation(out=dst[:, split:], in_=src[:, split:], func=ACT.Copy)

@@ -84,7 +84,10 @@ def tile_picked_yminp_sq_p_kernel(tc, x_words, x_scales, hT, offs, out):
             if (i, g) == (1, PASSES - 1):
                 nc.vector.tensor_copy(out=dst, in_=src)
                 return
-            split = LAST_ON_VECTOR // RUN if i == TILES - 1 else 0
+            if (i, g) == (TILES - 1, PASSES - 1):
+                nc.vector.tensor_copy(out=dst, in_=src)
+                return
+            split = 48 // RUN if i == TILES - 1 else 0
             if split:
                 nc.vector.tensor_copy(out=dst[:, :split], in_=src[:, :split])
             nc.scalar.activation(out=dst[:, split:], in_=src[:, split:], func=ACT.Copy)
@@ -131,8 +134,14 @@ def tile_picked_yminp_sq_p_kernel(tc, x_words, x_scales, hT, offs, out):
 
         def threshold(i):
             kept = new("kept", i, [P, S], F32)
+            exps = made["exps", i]
+            if len(spans[i]) > 1:
+                nc.scalar.activation(
+                    out=kept[:, spans[i][0]], in_=exps[:, spans[i][0]], func=ACT.Relu, bias=-SHARE, scale=1.0
+                )
+            cols = spans[i][-1]
             nc.vector.tensor_scalar(
-                out=kept[:], in0=made["exps", i][:], scalar1=-SHARE, scalar2=0.0, op0=ALU.add, op1=ALU.max
+                out=kept[:, cols], in0=exps[:, cols], scalar1=-SHARE, scalar2=0.0, op0=ALU.add, op1=ALU.max
             )
 
         def square(i):

@@ -23,7 +23,7 @@ PASSES = K // K_PASS
 TILES = V // P
 QUADRANTS, QUADRANT = 4, 32
 SCALE_ROWS = 4
-RUN = 4
+RUN = 2
 SHARE = 0.01
 LAST_ON_VECTOR = 88
 ALIGN = 64
@@ -87,7 +87,7 @@ def tile_picked_yminp_sq_p_kernel(tc, x_words, x_scales, hT, offs, out):
             if (i, g) == (TILES - 1, PASSES - 1):
                 nc.vector.tensor_copy(out=dst, in_=src)
                 return
-            split = 48 // RUN if i == TILES - 1 else 0
+            split = LAST_ON_VECTOR // RUN if i == TILES - 1 else 0
             if split:
                 nc.vector.tensor_copy(out=dst[:, :split], in_=src[:, :split])
             nc.scalar.activation(out=dst[:, split:], in_=src[:, split:], func=ACT.Copy)

@@ -158,13 +158,23 @@ def tile_picked_yminp_sq_p_kernel(tc, x_words, x_scales, hT, offs, out):
             for part in range(parts):
                 cols = slice(part * S // parts, (part + 1) * S // parts)
                 result = new("result", f"{i}_{part}", [P, S // parts], F32)
-                nc.vector.tensor_scalar(
-                    out=result[:],
-                    in0=made["squares", i][:, cols],
-                    scalar1=made["inverse", i][:],
-                    scalar2=None,
-                    op0=ALU.mult,
-                )
+                if i == 0:
+                    nc.gpsimd.tensor_scalar(
+                        out=result[:],
+                        in0=made["squares", i][:, cols],
+                        scalar1=made["inverse", i][:],
+                        scalar2=0.0,
+                        op0=ALU.mult,
+                        op1=ALU.add,
+                    )
+                else:
+                    nc.vector.tensor_scalar(
+                        out=result[:],
+                        in0=made["squares", i][:, cols],
+                        scalar1=made["inverse", i][:],
+                        scalar2=None,
+                        op0=ALU.mult,
+                    )
                 nc.sync.dma_start(out=out[i * P : (i + 1) * P, cols], in_=result[:])
 
         load_hidden(0, 0)

@@ -57,7 +57,8 @@ def tile_picked_yminp_sq_p_kernel(tc, x_words, x_scales, hT, offs, out):
 
         def load_scales():
             for q in range(QUADRANTS):
-                nc.sync.dma_start(
+                queue = nc.sync if q < QUADRANTS // 2 else nc.gpsimd
+                queue.dma_start(
                     out=table_scales[QUADRANT * q : QUADRANT * q + SCALE_ROWS * PASSES, :].bitcast(I32),
                     in_=x_scales[:, SCALE_ROWS * q : SCALE_ROWS * (q + 1), :].bitcast(I32),
                 )
@@ -177,17 +178,17 @@ def tile_picked_yminp_sq_p_kernel(tc, x_words, x_scales, hT, offs, out):
                     )
                 nc.sync.dma_start(out=out[i * P : (i + 1) * P, cols], in_=result[:])
 
+        load_words(0)
         load_hidden(0, 0)
         load_scales()
-        load_words(0)
         load_hidden(0, 1)
         load_words(1)
         for block in range(PASSES, TILES * PASSES):
             load_hidden(block // PASSES, block % PASSES)
 
-        nc.vector.tensor_copy(out=picked_scales[:], in_=table_scales[:].indirect(offsets[:]))
-        interleave(0, 0)
         gather_words(0)
+        interleave(0, 0)
+        nc.vector.tensor_copy(out=picked_scales[:], in_=table_scales[:].indirect(offsets[:]))
         quantize(0, 0)
         interleave(0, 1)
         quantize(0, 1)

@@ -15,6 +15,7 @@ FP8X4 = mybir.dt.float8_e4m3fn_x4
 ALU = mybir.AluOpType
 ACT = mybir.ActivationFunctionType
 AXIS = mybir.AxisListType
+BYTES_OF = {F32: 4, BF16: 2, I32: 4, U32: 4, U8: 1}
 
 P = 128
 PACK = 4
@@ -25,31 +26,37 @@ QUADRANTS, QUADRANT = 4, 32
 SCALE_ROWS = 4
 RUN = 2
 SHARE = 0.01
-LAST_ON_VECTOR = 88
 ALIGN = 64
-
-LAG_EXP, LAG_THRESHOLD, LAG_SQUARE, LAG_STORE = 1, 2, 3, 4
+SCALES_ON_SYNC = 4
 
 
 def tile_picked_yminp_sq_p_kernel(tc, x_words, x_scales, hT, offs, out):
     nc = tc.nc
     with ExitStack() as ctx:
+        held = ctx.enter_context(tc.tile_pool(name="held", bufs=1))
         sbuf = ctx.enter_context(tc.tile_pool(name="sbuf", bufs=1))
         psum = ctx.enter_context(tc.psum_pool(name="psum", bufs=1))
-        made = {}
+        made, start_of, free, left_to_take = {}, {}, [0], {}
 
-        def new(kind, key, shape, dtype, tag=None):
-            name = f"{kind}_{key}"
-            made[kind, key] = sbuf.tile(shape, dtype, name=name, tag=tag or name, align_bytes=ALIGN)
-            return made[kind, key]
+        def new(name, shape, dtype, over=None, at=0, room=0):
+            size = BYTES_OF[dtype]
+            for extent in shape[1:]:
+                size = size * extent
+            if over is None:
+                start_of[name] = free[0]
+                free[0] = free[0] + -(-max(size, room) // ALIGN) * ALIGN
+            else:
+                start_of[name] = start_of[over] + at
+            made[name] = sbuf.tile(shape, dtype, name=name, align_bytes=ALIGN, offset=start_of[name])
+            return made[name]
 
-        offsets = sbuf.tile([P, S // 16], U16, name="offsets")
+        offsets = held.tile([P, S // 16], U16, name="offsets")
         nc.sync.dma_start(offsets[:], offs)
 
-        table_scales = sbuf.tile([P, T], U8, name="table_scales", align_bytes=ALIGN)
+        table_scales = new("table_scales", [P, T], U8, room=4 * P + 4 * S)
         nc.gpsimd.memset(table_scales[:].bitcast(I32), 0)
-        picked_scales = sbuf.tile([P, S], U8, name="picked_scales", align_bytes=ALIGN)
-        spans = [[slice(h * S // 2, (h + 1) * S // 2) for h in range(2)]] + [[slice(0, S)]] * (TILES - 1)
+        halves = [slice(h * S // 2, (h + 1) * S // 2) for h in range(2)]
+        spans = [halves] + [[slice(0, S)]] * (TILES - 1)
         logits = [
             [psum.tile([P, cols.stop - cols.start], F32, name=f"logits_{i}_{cols.start}") for cols in spans[i]]
             for i in range(TILES)
@@ -57,158 +64,177 @@ def tile_picked_yminp_sq_p_kernel(tc, x_words, x_scales, hT, offs, out):
 
         def load_scales():
             for q in range(QUADRANTS):
-                queue = nc.sync if q < QUADRANTS // 2 else nc.gpsimd
+                queue = nc.sync if q < SCALES_ON_SYNC else nc.gpsimd
                 queue.dma_start(
                     out=table_scales[QUADRANT * q : QUADRANT * q + SCALE_ROWS * PASSES, :].bitcast(I32),
                     in_=x_scales[:, SCALE_ROWS * q : SCALE_ROWS * (q + 1), :].bitcast(I32),
                 )
 
         def load_words(g):
-            words = new("table_words", g, [P, T], I32)
+            words = new(f"table_words{g}", [P, T], I32)
             nc.sync.dma_start(out=words[:], in_=x_words[g].rearrange("p n j -> p (n j)").bitcast(I32))
 
         def load_hidden(i, g):
-            raw = new("raw", PASSES * i + g, [P, PACK, P], F32)
+            raw = new(f"raw{i}{g}", [P, PACK, P], F32)
             rows = hT[g * K_PASS : (g + 1) * K_PASS, i * P : (i + 1) * P]
             nc.sync.dma_start(out=raw[:], in_=rows.rearrange("(p j) c -> p j c", j=PACK))
 
-        def gather_words(g):
-            picked = new("picked_words", g, [P, S], U32)
-            for cols in spans[0] if g == PASSES - 1 else spans[1]:
-                entries = offsets[:, cols.start // 16 : cols.stop // 16]
-                nc.vector.tensor_copy(out=picked[:, cols], in_=made["table_words", g][:].bitcast(U32).indirect(entries))
+        def gather_scales():
+            picked = new("picked_scales", [P, S], U8)
+            nc.vector.tensor_copy(out=picked[:], in_=table_scales[:].indirect(offsets[:]))
 
-        def interleave(i, g):
-            grouped = new("grouped", PASSES * i + g, [P, P, PACK], BF16)
+        def gather_words(g, cols):
+            entries = offsets[:, cols.start // 16 : cols.stop // 16]
+            table = made[f"table_words{g}"]
+            nc.vector.tensor_copy(out=made[f"picked_words{g}"][:, cols], in_=table[:].bitcast(U32).indirect(entries))
+
+        def interleave(i, g, on_vector, over=None, at=0):
+            grouped = new(f"grouped{i}{g}", [P, P, PACK], BF16, over, at)
             dst = grouped[:].rearrange("p (c u) j -> p c j u", u=RUN)
-            src = made["raw", PASSES * i + g][:].rearrange("p j (c u) -> p c j u", u=RUN)
-            if (i, g) == (1, PASSES - 1):
-                nc.vector.tensor_copy(out=dst, in_=src)
-                return
-            if (i, g) == (TILES - 1, PASSES - 1):
-                nc.vector.tensor_copy(out=dst, in_=src)
-                return
-            split = LAST_ON_VECTOR // RUN if i == TILES - 1 else 0
-            if split:
+            src = made[f"raw{i}{g}"][:].rearrange("p j (c u) -> p c j u", u=RUN)
+            split = on_vector // RUN
+            if split > 0:
                 nc.vector.tensor_copy(out=dst[:, :split], in_=src[:, :split])
-            nc.scalar.activation(out=dst[:, split:], in_=src[:, split:], func=ACT.Copy)
+            if split < P // RUN:
+                nc.scalar.activation(out=dst[:, split:], in_=src[:, split:], func=ACT.Copy)
 
-        def quantize(i, g):
-            codes = new("codes", PASSES * i + g, [P, P], U32)
-            scales = new("scales", PASSES * i + g, [P, P], U8)
+        def quantize(i, g, over=None, at=0):
+            codes = new(f"codes{i}{g}", [P, P], U32, over, at)
+            scales = new(f"scales{i}{g}", [P, P], U8)
             nc.vector.quantize_mx(
                 out=codes[:].bitcast(FP8X4),
                 scales=scales[:],
-                in_=made["grouped", PASSES * i + g][:].rearrange("p c j -> p (c j)"),
+                in_=made[f"grouped{i}{g}"][:].rearrange("p c j -> p (c j)"),
             )
 
-        def multiply(i):
-            for g in range(PASSES):
-                for bank, cols in zip(logits[i], spans[i]):
-                    nc.tensor.matmul_mx(
-                        out=bank[:],
-                        lhsT=made["codes", PASSES * i + g][:].bitcast(FP8X4),
-                        lhsT_scale=made["scales", PASSES * i + g][:],
-                        rhs=made["picked_words", g][:, cols].bitcast(FP8X4),
-                        rhs_scale=picked_scales[SCALE_ROWS * g : P, cols],
-                        start=(g == 0),
-                        stop=(g == PASSES - 1),
-                    )
+        def multiply(i, g, part=0):
+            cols = spans[i][part]
+            nc.tensor.matmul_mx(
+                out=logits[i][part][:],
+                lhsT=made[f"codes{i}{g}"][:].bitcast(FP8X4),
+                lhsT_scale=made[f"scales{i}{g}"][:],
+                rhs=made[f"picked_words{g}"][:, cols].bitcast(FP8X4),
+                rhs_scale=made["picked_scales"][SCALE_ROWS * g : P, cols],
+                start=(g == 0),
+                stop=(g == PASSES - 1),
+            )
 
-        def row_max(i):
-            reuse = f"raw_{PASSES * (i + 2) - 1}" if i + 1 < TILES else None
-            neg_max = new("neg_max", i, [P, 1], F32, tag=reuse if len(logits[i]) == 1 else None)
-            if len(logits[i]) == 1:
-                nc.vector.tensor_reduce(out=neg_max[:], in_=logits[i][0][:], axis=AXIS.X, op=ALU.max, negate=True)
-                return
-            partial = new("partial_max", i, [P, len(logits[i])], F32, tag=reuse)
-            for h, bank in enumerate(logits[i]):
-                nc.vector.tensor_reduce(out=partial[:, h : h + 1], in_=bank[:], axis=AXIS.X, op=ALU.max)
-            nc.vector.tensor_reduce(out=neg_max[:], in_=partial[:], axis=AXIS.X, op=ALU.max, negate=True)
+        def row_max(i, over=None):
+            neg_max = new(f"neg_max{i}", [P, 1], F32, over, room=2 * K_PASS)
+            nc.vector.tensor_reduce(out=neg_max[:], in_=logits[i][0][:], axis=AXIS.X, op=ALU.max, negate=True)
 
-        def exponential(i):
-            exps = new("exps", i, [P, S], F32)
-            for bank, cols in zip(logits[i], spans[i]):
-                nc.scalar.activation(
-                    out=exps[:, cols], in_=bank[:], func=ACT.Exp, bias=made["neg_max", i][:], scale=1.0
-                )
+        def half_max(part, over=None):
+            partial = new(f"partial_max{part}", [P, 1], F32, over, ALIGN * part, room=2 * K_PASS)
+            nc.vector.tensor_reduce(out=partial[:], in_=logits[0][part][:], axis=AXIS.X, op=ALU.max)
 
-        def threshold(i):
-            kept = new("kept", i, [P, S], F32)
-            exps = made["exps", i]
-            if len(spans[i]) > 1:
-                nc.scalar.activation(
-                    out=kept[:, spans[i][0]], in_=exps[:, spans[i][0]], func=ACT.Relu, bias=-SHARE, scale=1.0
-                )
-            cols = spans[i][-1]
+        def join_max():
+            neg_max = new("neg_max0", [P, 1], F32, room=2 * K_PASS)
             nc.vector.tensor_scalar(
-                out=kept[:, cols], in0=exps[:, cols], scalar1=-SHARE, scalar2=0.0, op0=ALU.add, op1=ALU.max
+                out=neg_max[:],
+                in0=made["partial_max0"][:],
+                scalar1=made["partial_max1"][:],
+                scalar2=-1.0,
+                op0=ALU.max,
+                op1=ALU.mult,
             )
 
-        def square(i):
-            squares = new("squares", i, [P, S], F32)
-            total = new("total", i, [P, 1], F32)
-            nc.scalar.activation(out=squares[:], in_=made["kept", i][:], func=ACT.Square, accum_out=total[:])
+        def exponential(i, over=None):
+            exps = new(f"exps{i}", [P, S], F32, over)
+            for bank, cols in zip(logits[i], spans[i]):
+                nc.scalar.activation(out=exps[:, cols], in_=bank[:], func=ACT.Exp, bias=made[f"neg_max{i}"][:], scale=1.0)
+
+        def threshold(i, on_scalar=0, over=None):
+            kept = new(f"kept{i}", [P, S], F32, over)
+            exps = made[f"exps{i}"]
+            if on_scalar > 0:
+                nc.scalar.activation(
+                    out=kept[:, :on_scalar], in_=exps[:, :on_scalar], func=ACT.Relu, bias=-SHARE, scale=1.0
+                )
+            if on_scalar < S:
+                nc.vector.tensor_scalar(
+                    out=kept[:, on_scalar:], in0=exps[:, on_scalar:], scalar1=-SHARE, scalar2=0.0, op0=ALU.add, op1=ALU.max
+                )
+            left_to_take[i] = 0.0
+
+        def clamp(i, over=None):
+            kept = new(f"kept{i}", [P, S], F32, over)
+            nc.gpsimd.tensor_scalar(
+                out=kept[:], in0=made[f"exps{i}"][:], scalar1=1.0, scalar2=SHARE, op0=ALU.min, op1=ALU.max
+            )
+            left_to_take[i] = SHARE
+
+        def square(i, over=None):
+            squares = new(f"squares{i}", [P, S], F32, over)
+            total = new(f"total{i}", [P, 1], F32)
+            nc.scalar.activation(
+                out=squares[:],
+                in_=made[f"kept{i}"][:],
+                func=ACT.Square,
+                bias=-left_to_take[i],
+                scale=1.0,
+                accum_out=total[:],
+            )
 
         def invert_total(i):
-            inverse = new("inverse", i, [P, 1], F32)
-            nc.vector.reciprocal(out=inverse[:], in_=made["total", i][:])
+            inverse = new(f"inverse{i}", [P, 1], F32)
+            nc.vector.reciprocal(out=inverse[:], in_=made[f"total{i}"][:])
 
-        def normalise_and_store(i):
-            parts = 2 if i == TILES - 1 else 1
+        def normalise_and_store(i, engine, parts=1):
             for part in range(parts):
                 cols = slice(part * S // parts, (part + 1) * S // parts)
-                result = new("result", f"{i}_{part}", [P, S // parts], F32)
-                if i == 0:
-                    nc.gpsimd.tensor_scalar(
-                        out=result[:],
-                        in0=made["squares", i][:, cols],
-                        scalar1=made["inverse", i][:],
-                        scalar2=0.0,
-                        op0=ALU.mult,
-                        op1=ALU.add,
-                    )
+                result = new(f"result{i}{part}", [P, S // parts], F32)
+                squares, inverse = made[f"squares{i}"][:, cols], made[f"inverse{i}"][:]
+                if engine == "vector":
+                    nc.vector.tensor_scalar(out=result[:], in0=squares, scalar1=inverse, scalar2=None, op0=ALU.mult)
                 else:
-                    nc.vector.tensor_scalar(
-                        out=result[:],
-                        in0=made["squares", i][:, cols],
-                        scalar1=made["inverse", i][:],
-                        scalar2=None,
-                        op0=ALU.mult,
+                    nc.gpsimd.tensor_scalar(
+                        out=result[:], in0=squares, scalar1=inverse, scalar2=0.0, op0=ALU.mult, op1=ALU.add
                     )
                 nc.sync.dma_start(out=out[i * P : (i + 1) * P, cols], in_=result[:])
 
-        load_words(0)
         load_hidden(0, 0)
         load_scales()
+        load_words(0)
         load_hidden(0, 1)
         load_words(1)
         for block in range(PASSES, TILES * PASSES):
             load_hidden(block // PASSES, block % PASSES)
 
-        gather_words(0)
-        interleave(0, 0)
-        nc.vector.tensor_copy(out=picked_scales[:], in_=table_scales[:].indirect(offsets[:]))
+        gather_scales()
+        interleave(0, 0, 0)
+        new("picked_words0", [P, S], U32)
+        gather_words(0, slice(0, S))
         quantize(0, 0)
-        interleave(0, 1)
+        interleave(0, 1, 0)
         quantize(0, 1)
-        gather_words(1)
-        multiply(0)
-
-        def run(stage, i, *rest):
-            if 0 <= i < TILES:
-                stage(i, *rest)
-
+        new("picked_words1", [P, S], U32)
+        multiply(0, 0, 0)
+        multiply(0, 0, 1)
+        for part in range(2):
+            gather_words(1, halves[part])
+            multiply(0, 1, part)
+        on_vector = {(1, 1): P, (3, 0): 88, (3, 1): P}
         for n in range(1, TILES):
             for g in range(PASSES):
-                interleave(n, g)
+                interleave(n, g, on_vector.get((n, g), 0))
             for g in range(PASSES):
                 quantize(n, g)
-            multiply(n)
-        for n in range(1, TILES + LAG_STORE):
-            run(invert_total, n - LAG_STORE)
-            run(threshold, n - LAG_THRESHOLD)
-            run(row_max, n - LAG_EXP)
-            run(normalise_and_store, n - LAG_STORE)
-            run(exponential, n - LAG_EXP)
-            run(square, n - LAG_SQUARE)
+            for g in range(PASSES):
+                multiply(n, g)
+        for n in range(1, TILES + 4):
+            if 0 <= n - 4 < TILES:
+                invert_total(n - 4)
+            if 0 <= n - 2 < TILES:
+                threshold(n - 2, S // 2 if n == 2 else 0)
+            if n == 1:
+                half_max(0, "raw11")
+                half_max(1, "raw11")
+                join_max()
+            elif n - 1 < TILES:
+                row_max(n - 1, f"raw{n}1" if n < TILES else None)
+            if 0 <= n - 4 < TILES:
+                normalise_and_store(n - 4, "gpsimd" if n == 4 else "vector", 2 if n == TILES + 3 else 1)
+            if n - 1 < TILES:
+                exponential(n - 1)
+            if 0 <= n - 3 < TILES:
+                square(n - 3)

@@ -38,13 +38,13 @@ def tile_picked_yminp_sq_p_kernel(tc, x_words, x_scales, hT, offs, out):
         psum = ctx.enter_context(tc.psum_pool(name="psum", bufs=1))
         made, start_of, free, left_to_take = {}, {}, [0], {}
 
-        def new(name, shape, dtype, over=None, at=0, room=0):
+        def new(name, shape, dtype, over=None, at=0, room=0, lead=0):
             size = BYTES_OF[dtype]
             for extent in shape[1:]:
                 size = size * extent
             if over is None:
-                start_of[name] = free[0]
-                free[0] = free[0] + -(-max(size, room) // ALIGN) * ALIGN
+                start_of[name] = free[0] + lead
+                free[0] = start_of[name] + -(-max(size, room) // ALIGN) * ALIGN
             else:
                 start_of[name] = start_of[over] + at
             made[name] = sbuf.tile(shape, dtype, name=name, align_bytes=ALIGN, offset=start_of[name])
@@ -53,7 +53,7 @@ def tile_picked_yminp_sq_p_kernel(tc, x_words, x_scales, hT, offs, out):
         offsets = held.tile([P, S // 16], U16, name="offsets")
         nc.sync.dma_start(offsets[:], offs)
 
-        table_scales = new("table_scales", [P, T], U8, room=4 * P + 4 * S)
+        table_scales = new("table_scales", [P, T], U8, room=T + 4 * K_PASS, lead=4 * K_PASS)
         nc.gpsimd.memset(table_scales[:].bitcast(I32), 0)
         halves = [slice(h * S // 2, (h + 1) * S // 2) for h in range(2)]
         spans = [halves] + [[slice(0, S)]] * (TILES - 1)
@@ -74,8 +74,8 @@ def tile_picked_yminp_sq_p_kernel(tc, x_words, x_scales, hT, offs, out):
             words = new(f"table_words{g}", [P, T], I32)
             nc.sync.dma_start(out=words[:], in_=x_words[g].rearrange("p n j -> p (n j)").bitcast(I32))
 
-        def load_hidden(i, g):
-            raw = new(f"raw{i}{g}", [P, PACK, P], F32)
+        def load_hidden(i, g, over=None, at=0):
+            raw = new(f"raw{i}{g}", [P, PACK, P], F32, over, at)
             rows = hT[g * K_PASS : (g + 1) * K_PASS, i * P : (i + 1) * P]
             nc.sync.dma_start(out=raw[:], in_=rows.rearrange("(p j) c -> p j c", j=PACK))
 
@@ -88,6 +88,10 @@ def tile_picked_yminp_sq_p_kernel(tc, x_words, x_scales, hT, offs, out):
             table = made[f"table_words{g}"]
             nc.vector.tensor_copy(out=made[f"picked_words{g}"][:, cols], in_=table[:].bitcast(U32).indirect(entries))
 
+        def interleave_on_gpsimd(i, g, over=None, at=0):
+            grouped = new(f"grouped{i}{g}", [P, P, PACK], BF16, over, at)
+            nc.gpsimd.tensor_copy(out=grouped[:], in_=made[f"raw{i}{g}"][:].rearrange("p j c -> p c j"))
+
         def interleave(i, g, on_vector, over=None, at=0):
             grouped = new(f"grouped{i}{g}", [P, P, PACK], BF16, over, at)
             dst = grouped[:].rearrange("p (c u) j -> p c j u", u=RUN)
@@ -99,8 +103,8 @@ def tile_picked_yminp_sq_p_kernel(tc, x_words, x_scales, hT, offs, out):
                 nc.scalar.activation(out=dst[:, split:], in_=src[:, split:], func=ACT.Copy)
 
         def quantize(i, g, over=None, at=0):
-            codes = new(f"codes{i}{g}", [P, P], U32, over, at)
-            scales = new(f"scales{i}{g}", [P, P], U8)
+            codes = new(f"codes{i}{g}", [P, P], U32, room=4 * S)
+            scales = new(f"scales{i}{g}", [P, P], U8, over, at)
             nc.vector.quantize_mx(
                 out=codes[:].bitcast(FP8X4),
                 scales=scales[:],
@@ -120,15 +124,15 @@ def tile_picked_yminp_sq_p_kernel(tc, x_words, x_scales, hT, offs, out):
             )
 
         def row_max(i, over=None):
-            neg_max = new(f"neg_max{i}", [P, 1], F32, over, room=2 * K_PASS)
+            neg_max = new(f"neg_max{i}", [P, 1], F32, over, room=4 * S)
             nc.vector.tensor_reduce(out=neg_max[:], in_=logits[i][0][:], axis=AXIS.X, op=ALU.max, negate=True)
 
         def half_max(part, over=None):
-            partial = new(f"partial_max{part}", [P, 1], F32, over, ALIGN * part, room=2 * K_PASS)
+            partial = new(f"partial_max{part}", [P, 1], F32, over, room=4 * S)
             nc.vector.tensor_reduce(out=partial[:], in_=logits[0][part][:], axis=AXIS.X, op=ALU.max)
 
-        def join_max():
-            neg_max = new("neg_max0", [P, 1], F32, room=2 * K_PASS)
+        def join_max(over=None):
+            neg_max = new("neg_max0", [P, 1], F32, over, ALIGN, room=2 * K_PASS)
             nc.vector.tensor_scalar(
                 out=neg_max[:],
                 in0=made["partial_max0"][:],
@@ -175,14 +179,43 @@ def tile_picked_yminp_sq_p_kernel(tc, x_words, x_scales, hT, offs, out):
                 accum_out=total[:],
             )
 
+        def square_on_vector(i, over=None):
+            squares = new(f"squares{i}", [P, S], F32, over)
+            total = new(f"total{i}", [P, 1], F32)
+            kept = made[f"kept{i}"]
+            nc.vector.scalar_tensor_tensor(
+                out=squares[:], in0=kept[:], scalar=1.0, in1=kept[:], op0=ALU.mult, op1=ALU.mult, accum_out=total[:]
+            )
+
+        def square_shared(i, on_scalar, over=None):
+            squares = new(f"squares{i}", [P, S], F32, over)
+            partial = new(f"partial_total{i}", [P, 2], F32)
+            kept = made[f"kept{i}"]
+            nc.scalar.activation(
+                out=squares[:, :on_scalar], in_=kept[:, :on_scalar], func=ACT.Square, accum_out=partial[:, 0:1]
+            )
+            nc.vector.scalar_tensor_tensor(
+                out=squares[:, on_scalar:],
+                in0=kept[:, on_scalar:],
+                scalar=1.0,
+                in1=kept[:, on_scalar:],
+                op0=ALU.mult,
+                op1=ALU.mult,
+                accum_out=partial[:, 1:2],
+            )
+
+        def join_total(i):
+            total = new(f"total{i}", [P, 1], F32)
+            nc.vector.tensor_reduce(out=total[:], in_=made[f"partial_total{i}"][:], axis=AXIS.X, op=ALU.add)
+
         def invert_total(i):
             inverse = new(f"inverse{i}", [P, 1], F32)
             nc.vector.reciprocal(out=inverse[:], in_=made[f"total{i}"][:])
 
-        def normalise_and_store(i, engine, parts=1):
+        def normalise_and_store(i, engine, parts=1, over=None):
             for part in range(parts):
                 cols = slice(part * S // parts, (part + 1) * S // parts)
-                result = new(f"result{i}{part}", [P, S // parts], F32)
+                result = new(f"result{i}{part}", [P, S // parts], F32, over, part * 4 * S // parts)
                 squares, inverse = made[f"squares{i}"][:, cols], made[f"inverse{i}"][:]
                 if engine == "vector":
                     nc.vector.tensor_scalar(out=result[:], in0=squares, scalar1=inverse, scalar2=None, op0=ALU.mult)
@@ -223,18 +256,23 @@ def tile_picked_yminp_sq_p_kernel(tc, x_words, x_scales, hT, offs, out):
                 multiply(n, g)
         for n in range(1, TILES + 4):
             if 0 <= n - 4 < TILES:
+                if n == 5:
+                    join_total(1)
                 invert_total(n - 4)
             if 0 <= n - 2 < TILES:
                 threshold(n - 2, S // 2 if n == 2 else 0)
             if n == 1:
                 half_max(0, "raw11")
-                half_max(1, "raw11")
+                half_max(1, "grouped10")
                 join_max()
             elif n - 1 < TILES:
                 row_max(n - 1, f"raw{n}1" if n < TILES else None)
             if 0 <= n - 4 < TILES:
-                normalise_and_store(n - 4, "gpsimd" if n == 4 else "vector", 2 if n == TILES + 3 else 1)
+                normalise_and_store(n - 4, "vector", 2 if n >= TILES + 2 else 1, "neg_max3" if n == 5 else None)
             if n - 1 < TILES:
                 exponential(n - 1)
             if 0 <= n - 3 < TILES:
-                square(n - 3)
+                if n == 4:
+                    square_shared(1, S // 2, "codes31")
+                else:
+                    square(n - 3)

@@ -26,7 +26,7 @@ QUADRANTS, QUADRANT = 4, 32
 SCALE_ROWS = 4
 RUN = 2
 SHARE = 0.01
-ALIGN = 64
+ALIGN = 256
 SCALES_ON_SYNC = 4
 
 

@@ -15,7 +15,6 @@ FP8X4 = mybir.dt.float8_e4m3fn_x4
 ALU = mybir.AluOpType
 ACT = mybir.ActivationFunctionType
 AXIS = mybir.AxisListType
-BYTES_OF = {F32: 4, BF16: 2, I32: 4, U32: 4, U8: 1}
 
 P = 128
 PACK = 4
@@ -27,7 +26,8 @@ SCALE_ROWS = 4
 RUN = 2
 SHARE = 0.01
 ALIGN = 256
-SCALES_ON_SYNC = 4
+WHOLE = slice(0, S)
+HALVES = [slice(0, S // 2), slice(S // 2, S)]
 
 
 def tile_picked_yminp_sq_p_kernel(tc, x_words, x_scales, hT, offs, out):
@@ -36,85 +36,86 @@ def tile_picked_yminp_sq_p_kernel(tc, x_words, x_scales, hT, offs, out):
         held = ctx.enter_context(tc.tile_pool(name="held", bufs=1))
         sbuf = ctx.enter_context(tc.tile_pool(name="sbuf", bufs=1))
         psum = ctx.enter_context(tc.psum_pool(name="psum", bufs=1))
-        made, start_of, free, left_to_take = {}, {}, [0], {}
+        made, tag_of, logits = {}, {}, {}
 
-        def new(name, shape, dtype, over=None, at=0, room=0, lead=0):
-            size = BYTES_OF[dtype]
-            for extent in shape[1:]:
-                size = size * extent
-            if over is None:
-                start_of[name] = free[0] + lead
-                free[0] = start_of[name] + -(-max(size, room) // ALIGN) * ALIGN
-            else:
-                start_of[name] = start_of[over] + at
-            made[name] = sbuf.tile(shape, dtype, name=name, align_bytes=ALIGN, offset=start_of[name])
+        def new(name, shape, dtype, over=None):
+            tag_of[name] = name if over is None else tag_of[over]
+            made[name] = sbuf.tile(shape, dtype, name=name, tag=tag_of[name], align_bytes=ALIGN)
             return made[name]
 
-        offsets = held.tile([P, S // 16], U16, name="offsets")
-        nc.sync.dma_start(offsets[:], offs)
+        def load_list():
+            made["offsets"] = held.tile([P, S // 16], U16, name="offsets")
+            nc.sync.dma_start(made["offsets"][:], offs)
 
-        table_scales = new("table_scales", [P, T], U8, room=T + 4 * K_PASS, lead=4 * K_PASS)
-        nc.gpsimd.memset(table_scales[:].bitcast(I32), 0)
-        halves = [slice(h * S // 2, (h + 1) * S // 2) for h in range(2)]
-        spans = [halves] + [[slice(0, S)]] * (TILES - 1)
-        logits = [
-            [psum.tile([P, cols.stop - cols.start], F32, name=f"logits_{i}_{cols.start}") for cols in spans[i]]
-            for i in range(TILES)
-        ]
+        def clear_scales(engine=nc.gpsimd):
+            engine.memset(new("table_scales", [P, T], U8)[:].bitcast(I32), 0)
 
-        def load_scales():
+        def make_bias():
+            zero = new("zero", [P, 1], F32)
+            nc.gpsimd.memset(zero[:], 0.0)
+            nc.scalar.activation(out=new("neg_share", [P, 1], F32)[:], in_=zero[:], func=ACT.Identity, bias=-SHARE)
+
+        def load_scales(on_sync=QUADRANTS):
             for q in range(QUADRANTS):
-                queue = nc.sync if q < SCALES_ON_SYNC else nc.gpsimd
+                queue = nc.sync if q < on_sync else nc.scalar
                 queue.dma_start(
-                    out=table_scales[QUADRANT * q : QUADRANT * q + SCALE_ROWS * PASSES, :].bitcast(I32),
+                    out=made["table_scales"][QUADRANT * q : QUADRANT * q + SCALE_ROWS * PASSES, :].bitcast(I32),
                     in_=x_scales[:, SCALE_ROWS * q : SCALE_ROWS * (q + 1), :].bitcast(I32),
                 )
 
-        def load_words(g):
+        def load_words(g, parts=1):
             words = new(f"table_words{g}", [P, T], I32)
-            nc.sync.dma_start(out=words[:], in_=x_words[g].rearrange("p n j -> p (n j)").bitcast(I32))
+            rows = x_words[g].rearrange("p n j -> p (n j)").bitcast(I32)
+            for part in range(parts):
+                cols = slice(part * T // parts, (part + 1) * T // parts)
+                nc.sync.dma_start(out=words[:, cols], in_=rows[:, cols])
 
-        def load_hidden(i, g, over=None, at=0):
-            raw = new(f"raw{i}{g}", [P, PACK, P], F32, over, at)
-            rows = hT[g * K_PASS : (g + 1) * K_PASS, i * P : (i + 1) * P]
-            nc.sync.dma_start(out=raw[:], in_=rows.rearrange("(p j) c -> p j c", j=PACK))
+        def load_hidden(first, count, g, over=None, queue=nc.sync):
+            raw = new(f"raw{first}{g}", [P, PACK, count * P], F32, over)
+            rows = hT[g * K_PASS : (g + 1) * K_PASS, first * P : (first + count) * P]
+            queue.dma_start(out=raw[:], in_=rows.rearrange("(p j) c -> p j c", j=PACK))
+            for i in range(count):
+                made[f"slab{first + i}{g}"] = raw[:, :, i * P : (i + 1) * P]
 
         def gather_scales():
             picked = new("picked_scales", [P, S], U8)
-            nc.vector.tensor_copy(out=picked[:], in_=table_scales[:].indirect(offsets[:]))
+            nc.vector.tensor_copy(out=picked[:], in_=made["table_scales"][:].indirect(made["offsets"][:]))
 
-        def gather_words(g, cols):
-            entries = offsets[:, cols.start // 16 : cols.stop // 16]
+        def gather_words(g, cols=WHOLE, over=None):
+            if cols.start == 0:
+                new(f"picked_words{g}", [P, S], U32, over)
+            entries = made["offsets"][:, cols.start // 16 : cols.stop // 16]
             table = made[f"table_words{g}"]
             nc.vector.tensor_copy(out=made[f"picked_words{g}"][:, cols], in_=table[:].bitcast(U32).indirect(entries))
 
-        def interleave_on_gpsimd(i, g, over=None, at=0):
-            grouped = new(f"grouped{i}{g}", [P, P, PACK], BF16, over, at)
-            nc.gpsimd.tensor_copy(out=grouped[:], in_=made[f"raw{i}{g}"][:].rearrange("p j c -> p c j"))
-
-        def interleave(i, g, on_vector, over=None, at=0):
-            grouped = new(f"grouped{i}{g}", [P, P, PACK], BF16, over, at)
+        def interleave(i, g, on_vector=0, over=None):
+            grouped = new(f"grouped{i}{g}", [P, P, PACK], BF16, over)
             dst = grouped[:].rearrange("p (c u) j -> p c j u", u=RUN)
-            src = made[f"raw{i}{g}"][:].rearrange("p j (c u) -> p c j u", u=RUN)
+            src = made[f"slab{i}{g}"].rearrange("p j (c u) -> p c j u", u=RUN)
             split = on_vector // RUN
             if split > 0:
                 nc.vector.tensor_copy(out=dst[:, :split], in_=src[:, :split])
             if split < P // RUN:
                 nc.scalar.activation(out=dst[:, split:], in_=src[:, split:], func=ACT.Copy)
 
-        def quantize(i, g, over=None, at=0):
-            codes = new(f"codes{i}{g}", [P, P], U32, room=4 * S)
-            scales = new(f"scales{i}{g}", [P, P], U8, over, at)
+        def interleave_on_gpsimd(i, g, over=None):
+            grouped = new(f"grouped{i}{g}", [P, P, PACK], BF16, over)
+            nc.gpsimd.tensor_copy(out=grouped[:], in_=made[f"slab{i}{g}"].rearrange("p j c -> p c j"))
+
+        def quantize(i, g, over=None):
+            codes = new(f"codes{i}{g}", [P, P], U32, over)
+            scales = new(f"scales{i}{g}", [P, P], U8)
             nc.vector.quantize_mx(
                 out=codes[:].bitcast(FP8X4),
                 scales=scales[:],
                 in_=made[f"grouped{i}{g}"][:].rearrange("p c j -> p (c j)"),
             )
 
-        def multiply(i, g, part=0):
-            cols = spans[i][part]
+        def multiply(i, g, cols=WHOLE):
+            if g == 0:
+                logits[i, cols.start] = psum.tile([P, cols.stop - cols.start], F32, name=f"logits_{i}_{cols.start}")
             nc.tensor.matmul_mx(
-                out=logits[i][part][:],
+                out=logits[i, cols.start][:],
                 lhsT=made[f"codes{i}{g}"][:].bitcast(FP8X4),
                 lhsT_scale=made[f"scales{i}{g}"][:],
                 rhs=made[f"picked_words{g}"][:, cols].bitcast(FP8X4),
@@ -123,60 +124,62 @@ def tile_picked_yminp_sq_p_kernel(tc, x_words, x_scales, hT, offs, out):
                 stop=(g == PASSES - 1),
             )
 
+        def max_columns(tiles, over):
+            shared = new(f"neg_max_from{tiles[0]}", [P, len(tiles)], F32, over)
+            for column, i in enumerate(tiles):
+                made[f"neg_max{i}"] = shared[:, column : column + 1]
+
         def row_max(i, over=None):
-            neg_max = new(f"neg_max{i}", [P, 1], F32, over, room=4 * S)
-            nc.vector.tensor_reduce(out=neg_max[:], in_=logits[i][0][:], axis=AXIS.X, op=ALU.max, negate=True)
+            neg_max = made[f"neg_max{i}"] if f"neg_max{i}" in made else new(f"neg_max{i}", [P, 1], F32, over)
+            nc.vector.tensor_reduce(out=neg_max[:], in_=logits[i, 0][:], axis=AXIS.X, op=ALU.max, negate=True)
 
-        def half_max(part, over=None):
-            partial = new(f"partial_max{part}", [P, 1], F32, over, room=4 * S)
-            nc.vector.tensor_reduce(out=partial[:], in_=logits[0][part][:], axis=AXIS.X, op=ALU.max)
+        def half_max(i, part, over=None):
+            partial = new(f"partial_max{i}{part}", [P, 1], F32, over)
+            nc.vector.tensor_reduce(out=partial[:], in_=logits[i, HALVES[part].start][:], axis=AXIS.X, op=ALU.max)
 
-        def join_max(over=None):
-            neg_max = new("neg_max0", [P, 1], F32, over, ALIGN, room=2 * K_PASS)
+        def join_max(i, over=None):
+            neg_max = made[f"neg_max{i}"] if f"neg_max{i}" in made else new(f"neg_max{i}", [P, 1], F32, over)
             nc.vector.tensor_scalar(
                 out=neg_max[:],
-                in0=made["partial_max0"][:],
-                scalar1=made["partial_max1"][:],
+                in0=made[f"partial_max{i}0"][:],
+                scalar1=made[f"partial_max{i}1"][:],
                 scalar2=-1.0,
                 op0=ALU.max,
                 op1=ALU.mult,
             )
 
-        def exponential(i, over=None):
-            exps = new(f"exps{i}", [P, S], F32, over)
-            for bank, cols in zip(logits[i], spans[i]):
-                nc.scalar.activation(out=exps[:, cols], in_=bank[:], func=ACT.Exp, bias=made[f"neg_max{i}"][:], scale=1.0)
+        def exponential(i, cols=WHOLE, over=None):
+            if cols.start == 0:
+                new(f"exps{i}", [P, S], F32, over)
+            bank = logits[i, cols.start][:] if (i, cols.start) in logits else logits[i, 0][:, cols.start :]
+            nc.scalar.activation(
+                out=made[f"exps{i}"][:, cols],
+                in_=bank[:, : cols.stop - cols.start],
+                func=ACT.Exp,
+                bias=made[f"neg_max{i}"][:],
+                scale=1.0,
+            )
 
-        def threshold(i, on_scalar=0, over=None):
-            kept = new(f"kept{i}", [P, S], F32, over)
-            exps = made[f"exps{i}"]
-            if on_scalar > 0:
-                nc.scalar.activation(
-                    out=kept[:, :on_scalar], in_=exps[:, :on_scalar], func=ACT.Relu, bias=-SHARE, scale=1.0
-                )
-            if on_scalar < S:
-                nc.vector.tensor_scalar(
-                    out=kept[:, on_scalar:], in0=exps[:, on_scalar:], scalar1=-SHARE, scalar2=0.0, op0=ALU.add, op1=ALU.max
-                )
-            left_to_take[i] = 0.0
+        def threshold(i, cols=WHOLE, engine="vector", over=None):
+            if f"kept{i}" not in made:
+                new(f"kept{i}", [P, S], F32, over)
+            kept, exps = made[f"kept{i}"][:, cols], made[f"exps{i}"][:, cols]
+            if engine == "scalar":
+                nc.scalar.activation(out=kept, in_=exps, func=ACT.Relu, bias=made["neg_share"][:] if "neg_share" in made else -SHARE, scale=1.0)
+            else:
+                nc.vector.tensor_scalar(out=kept, in0=exps, scalar1=-SHARE, scalar2=0.0, op0=ALU.add, op1=ALU.max)
 
         def clamp(i, over=None):
             kept = new(f"kept{i}", [P, S], F32, over)
             nc.gpsimd.tensor_scalar(
                 out=kept[:], in0=made[f"exps{i}"][:], scalar1=1.0, scalar2=SHARE, op0=ALU.min, op1=ALU.max
             )
-            left_to_take[i] = SHARE
 
-        def square(i, over=None):
+        def square(i, take=0.0, over=None):
             squares = new(f"squares{i}", [P, S], F32, over)
             total = new(f"total{i}", [P, 1], F32)
             nc.scalar.activation(
-                out=squares[:],
-                in_=made[f"kept{i}"][:],
-                func=ACT.Square,
-                bias=-left_to_take[i],
-                scale=1.0,
-                accum_out=total[:],
+                out=squares[:], in_=made[f"kept{i}"][:], func=ACT.Square, bias=-take, scale=1.0, accum_out=total[:]
             )
 
         def square_on_vector(i, over=None):
@@ -187,22 +190,19 @@ def tile_picked_yminp_sq_p_kernel(tc, x_words, x_scales, hT, offs, out):
                 out=squares[:], in0=kept[:], scalar=1.0, in1=kept[:], op0=ALU.mult, op1=ALU.mult, accum_out=total[:]
             )
 
-        def square_shared(i, on_scalar, over=None):
-            squares = new(f"squares{i}", [P, S], F32, over)
-            partial = new(f"partial_total{i}", [P, 2], F32)
-            kept = made[f"kept{i}"]
-            nc.scalar.activation(
-                out=squares[:, :on_scalar], in_=kept[:, :on_scalar], func=ACT.Square, accum_out=partial[:, 0:1]
-            )
-            nc.vector.scalar_tensor_tensor(
-                out=squares[:, on_scalar:],
-                in0=kept[:, on_scalar:],
-                scalar=1.0,
-                in1=kept[:, on_scalar:],
-                op0=ALU.mult,
-                op1=ALU.mult,
-                accum_out=partial[:, 1:2],
-            )
+        def square_half(i, part, engine, over=None, cut=S // 2):
+            if f"squares{i}" not in made:
+                new(f"squares{i}", [P, S], F32, over)
+                new(f"partial_total{i}", [P, 2], F32)
+            cols = [slice(0, cut), slice(cut, S)][part]
+            squares, kept = made[f"squares{i}"][:, cols], made[f"kept{i}"][:, cols]
+            partial = made[f"partial_total{i}"][:, part : part + 1]
+            if engine == "scalar":
+                nc.scalar.activation(out=squares, in_=kept, func=ACT.Square, accum_out=partial)
+            else:
+                nc.vector.scalar_tensor_tensor(
+                    out=squares, in0=kept, scalar=1.0, in1=kept, op0=ALU.mult, op1=ALU.mult, accum_out=partial
+                )
 
         def join_total(i):
             total = new(f"total{i}", [P, 1], F32)
@@ -212,67 +212,78 @@ def tile_picked_yminp_sq_p_kernel(tc, x_words, x_scales, hT, offs, out):
             inverse = new(f"inverse{i}", [P, 1], F32)
             nc.vector.reciprocal(out=inverse[:], in_=made[f"total{i}"][:])
 
-        def normalise_and_store(i, engine, parts=1, over=None):
-            for part in range(parts):
+        def normalise_and_store(i, parts=1, engine="vector", over=None, only=None):
+            for part in range(parts) if only is None else [only]:
                 cols = slice(part * S // parts, (part + 1) * S // parts)
-                result = new(f"result{i}{part}", [P, S // parts], F32, over, part * 4 * S // parts)
+                result = new(f"result{i}{part}", [P, S // parts], F32, over if part == (only or 0) else None)
                 squares, inverse = made[f"squares{i}"][:, cols], made[f"inverse{i}"][:]
                 if engine == "vector":
                     nc.vector.tensor_scalar(out=result[:], in0=squares, scalar1=inverse, scalar2=None, op0=ALU.mult)
+                elif engine == "scalar":
+                    nc.scalar.activation(out=result[:], in_=squares, func=ACT.Copy, scale=inverse)
                 else:
                     nc.gpsimd.tensor_scalar(
                         out=result[:], in0=squares, scalar1=inverse, scalar2=0.0, op0=ALU.mult, op1=ALU.add
                     )
                 nc.sync.dma_start(out=out[i * P : (i + 1) * P, cols], in_=result[:])
 
-        load_hidden(0, 0)
+        load_list()
+        clear_scales()
+        load_hidden(0, 1, 0)
         load_scales()
         load_words(0)
-        load_hidden(0, 1)
+        load_hidden(0, 1, 1)
         load_words(1)
-        for block in range(PASSES, TILES * PASSES):
-            load_hidden(block // PASSES, block % PASSES)
+        for i in range(1, TILES):
+            for g in range(PASSES):
+                load_hidden(i, 1, g)
 
         gather_scales()
-        interleave(0, 0, 0)
-        new("picked_words0", [P, S], U32)
-        gather_words(0, slice(0, S))
+        interleave(0, 0)
+        gather_words(0)
         quantize(0, 0)
-        interleave(0, 1, 0)
+        interleave(0, 1)
         quantize(0, 1)
-        new("picked_words1", [P, S], U32)
-        multiply(0, 0, 0)
-        multiply(0, 0, 1)
-        for part in range(2):
-            gather_words(1, halves[part])
-            multiply(0, 1, part)
-        on_vector = {(1, 1): P, (3, 0): 88, (3, 1): P}
-        for n in range(1, TILES):
+        for cols in HALVES:
+            multiply(0, 0, cols)
+        for cols in HALVES:
+            gather_words(1, cols)
+            multiply(0, 1, cols)
+        on_vector = {(1, 1): P, (3, 0): 48, (3, 1): P}
+        for i in range(1, TILES):
             for g in range(PASSES):
-                interleave(n, g, on_vector.get((n, g), 0))
+                interleave(i, g, on_vector.get((i, g), 0))
             for g in range(PASSES):
-                quantize(n, g)
+                quantize(i, g)
             for g in range(PASSES):
-                multiply(n, g)
-        for n in range(1, TILES + 4):
-            if 0 <= n - 4 < TILES:
-                if n == 5:
-                    join_total(1)
-                invert_total(n - 4)
-            if 0 <= n - 2 < TILES:
-                threshold(n - 2, S // 2 if n == 2 else 0)
-            if n == 1:
-                half_max(0, "raw11")
-                half_max(1, "grouped10")
-                join_max()
-            elif n - 1 < TILES:
-                row_max(n - 1, f"raw{n}1" if n < TILES else None)
-            if 0 <= n - 4 < TILES:
-                normalise_and_store(n - 4, "vector", 2 if n >= TILES + 2 else 1, "neg_max3" if n == 5 else None)
-            if n - 1 < TILES:
-                exponential(n - 1)
-            if 0 <= n - 3 < TILES:
-                if n == 4:
-                    square_shared(1, S // 2, "codes31")
-                else:
-                    square(n - 3)
+                multiply(i, g)
+        half_max(0, 0, "raw11")
+        half_max(0, 1, "grouped10")
+        join_max(0)
+        for cols in HALVES:
+            exponential(0, cols)
+        threshold(0, HALVES[0], "scalar")
+        threshold(0, HALVES[1])
+        row_max(1, "raw21")
+        exponential(1)
+        threshold(1)
+        row_max(2, "raw31")
+        exponential(2)
+        square(0)
+        invert_total(0)
+        threshold(2)
+        row_max(3)
+        normalise_and_store(0)
+        exponential(3)
+        square_half(1, 0, "scalar", "codes31")
+        square_half(1, 1, "vector")
+        join_total(1)
+        invert_total(1)
+        threshold(3)
+        normalise_and_store(1, over="neg_max3")
+        square(2)
+        invert_total(2)
+        normalise_and_store(2, 2)
+        square(3)
+        invert_total(3)
+        normalise_and_store(3, 2)

from contextlib import ExitStack

import concourse.mybir as mybir

K, T, S, V = 1024, 1024, 512, 512
FLOPS = 2 * K * S * V

F32 = mybir.dt.float32
BF16 = mybir.dt.bfloat16
I32 = mybir.dt.int32
U32 = mybir.dt.uint32
U16 = mybir.dt.uint16
U8 = mybir.dt.uint8
FP8X4 = mybir.dt.float8_e4m3fn_x4
ALU = mybir.AluOpType
ACT = mybir.ActivationFunctionType
AXIS = mybir.AxisListType

P = 128
PACK = 4
K_PASS = P * PACK
PASSES = K // K_PASS
TILES = V // P
QUADRANTS, QUADRANT = 4, 32
SCALE_ROWS = 4
RUN = 2
SHARE = 0.01
ALIGN = 256
WHOLE = slice(0, S)
HALVES = [slice(0, S // 2), slice(S // 2, S)]


def tile_picked_yminp_sq_p_kernel(tc, x_words, x_scales, hT, offs, out):
    nc = tc.nc
    with ExitStack() as ctx:
        held = ctx.enter_context(tc.tile_pool(name="held", bufs=1))
        sbuf = ctx.enter_context(tc.tile_pool(name="sbuf", bufs=1))
        psum = ctx.enter_context(tc.psum_pool(name="psum", bufs=1))
        made, tag_of, logits = {}, {}, {}

        def new(name, shape, dtype, over=None):
            tag_of[name] = name if over is None else tag_of[over]
            made[name] = sbuf.tile(shape, dtype, name=name, tag=tag_of[name], align_bytes=ALIGN)
            return made[name]

        def load_list():
            made["offsets"] = held.tile([P, S // 16], U16, name="offsets")
            nc.sync.dma_start(made["offsets"][:], offs)

        def clear_scales(engine=nc.gpsimd):
            engine.memset(new("table_scales", [P, T], U8)[:].bitcast(I32), 0)

        def make_bias():
            zero = new("zero", [P, 1], F32)
            nc.gpsimd.memset(zero[:], 0.0)
            nc.scalar.activation(out=new("neg_share", [P, 1], F32)[:], in_=zero[:], func=ACT.Identity, bias=-SHARE)

        def load_scales(on_sync=QUADRANTS):
            for q in range(QUADRANTS):
                queue = nc.sync if q < on_sync else nc.scalar
                queue.dma_start(
                    out=made["table_scales"][QUADRANT * q : QUADRANT * q + SCALE_ROWS * PASSES, :].bitcast(I32),
                    in_=x_scales[:, SCALE_ROWS * q : SCALE_ROWS * (q + 1), :].bitcast(I32),
                )

        def load_words(g, parts=1):
            words = new(f"table_words{g}", [P, T], I32)
            rows = x_words[g].rearrange("p n j -> p (n j)").bitcast(I32)
            for part in range(parts):
                cols = slice(part * T // parts, (part + 1) * T // parts)
                nc.sync.dma_start(out=words[:, cols], in_=rows[:, cols])

        def load_hidden(first, count, g, over=None, queue=nc.sync):
            raw = new(f"raw{first}{g}", [P, PACK, count * P], F32, over)
            rows = hT[g * K_PASS : (g + 1) * K_PASS, first * P : (first + count) * P]
            queue.dma_start(out=raw[:], in_=rows.rearrange("(p j) c -> p j c", j=PACK))
            for i in range(count):
                made[f"slab{first + i}{g}"] = raw[:, :, i * P : (i + 1) * P]

        def gather_scales():
            picked = new("picked_scales", [P, S], U8)
            nc.vector.tensor_copy(out=picked[:], in_=made["table_scales"][:].indirect(made["offsets"][:]))

        def gather_words(g, cols=WHOLE, over=None):
            if cols.start == 0:
                new(f"picked_words{g}", [P, S], U32, over)
            entries = made["offsets"][:, cols.start // 16 : cols.stop // 16]
            table = made[f"table_words{g}"]
            nc.vector.tensor_copy(out=made[f"picked_words{g}"][:, cols], in_=table[:].bitcast(U32).indirect(entries))

        def interleave(i, g, on_vector=0, over=None):
            grouped = new(f"grouped{i}{g}", [P, P, PACK], BF16, over)
            dst = grouped[:].rearrange("p (c u) j -> p c j u", u=RUN)
            src = made[f"slab{i}{g}"].rearrange("p j (c u) -> p c j u", u=RUN)
            split = on_vector // RUN
            if split > 0:
                nc.vector.tensor_copy(out=dst[:, :split], in_=src[:, :split])
            if split < P // RUN:
                nc.scalar.activation(out=dst[:, split:], in_=src[:, split:], func=ACT.Copy)

        def interleave_on_gpsimd(i, g, over=None):
            grouped = new(f"grouped{i}{g}", [P, P, PACK], BF16, over)
            nc.gpsimd.tensor_copy(out=grouped[:], in_=made[f"slab{i}{g}"].rearrange("p j c -> p c j"))

        def quantize(i, g, over=None):
            codes = new(f"codes{i}{g}", [P, P], U32, over)
            scales = new(f"scales{i}{g}", [P, P], U8)
            nc.vector.quantize_mx(
                out=codes[:].bitcast(FP8X4),
                scales=scales[:],
                in_=made[f"grouped{i}{g}"][:].rearrange("p c j -> p (c j)"),
            )

        def multiply(i, g, cols=WHOLE):
            if g == 0:
                logits[i, cols.start] = psum.tile([P, cols.stop - cols.start], F32, name=f"logits_{i}_{cols.start}")
            nc.tensor.matmul_mx(
                out=logits[i, cols.start][:],
                lhsT=made[f"codes{i}{g}"][:].bitcast(FP8X4),
                lhsT_scale=made[f"scales{i}{g}"][:],
                rhs=made[f"picked_words{g}"][:, cols].bitcast(FP8X4),
                rhs_scale=made["picked_scales"][SCALE_ROWS * g : P, cols],
                start=(g == 0),
                stop=(g == PASSES - 1),
            )

        def max_columns(tiles, over):
            shared = new(f"neg_max_from{tiles[0]}", [P, len(tiles)], F32, over)
            for column, i in enumerate(tiles):
                made[f"neg_max{i}"] = shared[:, column : column + 1]

        def row_max(i, over=None):
            neg_max = made[f"neg_max{i}"] if f"neg_max{i}" in made else new(f"neg_max{i}", [P, 1], F32, over)
            nc.vector.tensor_reduce(out=neg_max[:], in_=logits[i, 0][:], axis=AXIS.X, op=ALU.max, negate=True)

        def half_max(i, part, over=None):
            partial = new(f"partial_max{i}{part}", [P, 1], F32, over)
            nc.vector.tensor_reduce(out=partial[:], in_=logits[i, HALVES[part].start][:], axis=AXIS.X, op=ALU.max)

        def join_max(i, over=None):
            neg_max = made[f"neg_max{i}"] if f"neg_max{i}" in made else new(f"neg_max{i}", [P, 1], F32, over)
            nc.vector.tensor_scalar(
                out=neg_max[:],
                in0=made[f"partial_max{i}0"][:],
                scalar1=made[f"partial_max{i}1"][:],
                scalar2=-1.0,
                op0=ALU.max,
                op1=ALU.mult,
            )

        def exponential(i, cols=WHOLE, over=None):
            if cols.start == 0:
                new(f"exps{i}", [P, S], F32, over)
            bank = logits[i, cols.start][:] if (i, cols.start) in logits else logits[i, 0][:, cols.start :]
            nc.scalar.activation(
                out=made[f"exps{i}"][:, cols],
                in_=bank[:, : cols.stop - cols.start],
                func=ACT.Exp,
                bias=made[f"neg_max{i}"][:],
                scale=1.0,
            )

        def threshold(i, cols=WHOLE, engine="vector", over=None):
            if f"kept{i}" not in made:
                new(f"kept{i}", [P, S], F32, over)
            kept, exps = made[f"kept{i}"][:, cols], made[f"exps{i}"][:, cols]
            if engine == "scalar":
                nc.scalar.activation(out=kept, in_=exps, func=ACT.Relu, bias=made["neg_share"][:] if "neg_share" in made else -SHARE, scale=1.0)
            else:
                nc.vector.tensor_scalar(out=kept, in0=exps, scalar1=-SHARE, scalar2=0.0, op0=ALU.add, op1=ALU.max)

        def clamp(i, over=None):
            kept = new(f"kept{i}", [P, S], F32, over)
            nc.gpsimd.tensor_scalar(
                out=kept[:], in0=made[f"exps{i}"][:], scalar1=1.0, scalar2=SHARE, op0=ALU.min, op1=ALU.max
            )

        def square(i, take=0.0, over=None):
            squares = new(f"squares{i}", [P, S], F32, over)
            total = new(f"total{i}", [P, 1], F32)
            nc.scalar.activation(
                out=squares[:], in_=made[f"kept{i}"][:], func=ACT.Square, bias=-take, scale=1.0, accum_out=total[:]
            )

        def square_on_vector(i, over=None):
            squares = new(f"squares{i}", [P, S], F32, over)
            total = new(f"total{i}", [P, 1], F32)
            kept = made[f"kept{i}"]
            nc.vector.scalar_tensor_tensor(
                out=squares[:], in0=kept[:], scalar=1.0, in1=kept[:], op0=ALU.mult, op1=ALU.mult, accum_out=total[:]
            )

        def square_half(i, part, engine, over=None, cut=S // 2):
            if f"squares{i}" not in made:
                new(f"squares{i}", [P, S], F32, over)
                new(f"partial_total{i}", [P, 2], F32)
            cols = [slice(0, cut), slice(cut, S)][part]
            squares, kept = made[f"squares{i}"][:, cols], made[f"kept{i}"][:, cols]
            partial = made[f"partial_total{i}"][:, part : part + 1]
            if engine == "scalar":
                nc.scalar.activation(out=squares, in_=kept, func=ACT.Square, accum_out=partial)
            else:
                nc.vector.scalar_tensor_tensor(
                    out=squares, in0=kept, scalar=1.0, in1=kept, op0=ALU.mult, op1=ALU.mult, accum_out=partial
                )

        def join_total(i):
            total = new(f"total{i}", [P, 1], F32)
            nc.vector.tensor_reduce(out=total[:], in_=made[f"partial_total{i}"][:], axis=AXIS.X, op=ALU.add)

        def invert_total(i):
            inverse = new(f"inverse{i}", [P, 1], F32)
            nc.vector.reciprocal(out=inverse[:], in_=made[f"total{i}"][:])

        def normalise_and_store(i, parts=1, engine="vector", over=None, only=None):
            for part in range(parts) if only is None else [only]:
                cols = slice(part * S // parts, (part + 1) * S // parts)
                result = new(f"result{i}{part}", [P, S // parts], F32, over if part == (only or 0) else None)
                squares, inverse = made[f"squares{i}"][:, cols], made[f"inverse{i}"][:]
                if engine == "vector":
                    nc.vector.tensor_scalar(out=result[:], in0=squares, scalar1=inverse, scalar2=None, op0=ALU.mult)
                elif engine == "scalar":
                    nc.scalar.activation(out=result[:], in_=squares, func=ACT.Copy, scale=inverse)
                else:
                    nc.gpsimd.tensor_scalar(
                        out=result[:], in0=squares, scalar1=inverse, scalar2=0.0, op0=ALU.mult, op1=ALU.add
                    )
                nc.sync.dma_start(out=out[i * P : (i + 1) * P, cols], in_=result[:])

        load_list()
        clear_scales()
        load_hidden(0, 1, 0)
        load_scales()
        load_words(0)
        load_hidden(0, 1, 1)
        load_words(1)
        for i in range(1, TILES):
            for g in range(PASSES):
                load_hidden(i, 1, g)

        gather_scales()
        interleave(0, 0)
        gather_words(0)
        quantize(0, 0)
        interleave(0, 1)
        quantize(0, 1)
        for cols in HALVES:
            multiply(0, 0, cols)
        for cols in HALVES:
            gather_words(1, cols)
            multiply(0, 1, cols)
        on_vector = {(1, 1): P, (3, 0): 48, (3, 1): P}
        for i in range(1, TILES):
            for g in range(PASSES):
                interleave(i, g, on_vector.get((i, g), 0))
            for g in range(PASSES):
                quantize(i, g)
            for g in range(PASSES):
                multiply(i, g)
        half_max(0, 0, "raw11")
        half_max(0, 1, "grouped10")
        join_max(0)
        for cols in HALVES:
            exponential(0, cols)
        threshold(0, HALVES[0], "scalar")
        threshold(0, HALVES[1])
        row_max(1, "raw21")
        exponential(1)
        threshold(1)
        row_max(2, "raw31")
        exponential(2)
        square(0)
        invert_total(0)
        threshold(2)
        row_max(3)
        normalise_and_store(0)
        exponential(3)
        square_half(1, 0, "scalar", "codes31")
        square_half(1, 1, "vector")
        join_total(1)
        invert_total(1)
        threshold(3)
        normalise_and_store(1, over="neg_max3")
        square(2)
        invert_total(2)
        normalise_and_store(2, 2)
        square(3)
        invert_total(3)
        normalise_and_store(3, 2)
